import numpy as np
import ml_dtypes


def mxq(x, axis, fmt="e4m3"):
    dtype, down = {"e4m3": (ml_dtypes.float8_e4m3fn, 7), "e5m2": (ml_dtypes.float8_e5m2, 14)}[fmt]
    v = np.moveaxis(np.asarray(x, np.float32).astype(ml_dtypes.bfloat16).astype(np.float64), axis, -1)
    blocks = v.reshape(v.shape[:-1] + (-1, 32))
    amax = np.abs(blocks).max(-1, keepdims=True)
    byte = np.maximum(np.where(amax > 0, np.frexp(amax)[1] - 1 + 127, 0) - down, 1)
    scale = np.exp2(byte - 127.0)
    codes = (blocks / scale).astype(np.float32).astype(dtype).astype(np.float64)
    return np.moveaxis((codes * scale).reshape(v.shape), -1, axis)


WIDE = False


def mx_kscale(k):
    if not WIDE:
        return np.ones(k)
    levels = np.array([10, -10, 5, -5, 0])
    if k % 512:
        return np.exp2(np.random.permutation(np.resize(levels, k // 32))).repeat(32)
    a = np.empty((k // 512, 16))
    for p in range(k // 512):
        a[p, :8] = np.random.permutation(np.resize(levels, 8))
        for g in range(8):
            far = levels[np.abs(levels - a[p, g]) >= 10]
            a[p, g + 8] = far[np.random.randint(len(far))]
    return np.exp2(a.ravel()).repeat(32)


def f64(x):
    return np.asarray(x).astype(np.float64)


def striped(idx):
    return np.tile(idx.reshape(-1, 16).T, (8, 1)).astype(np.uint16)


def unstriped(offs):
    return offs[:16].T.reshape(-1).astype(np.int64)


def pack_weight(w):
    k, n = w.shape
    w = f64(np.asarray(w, np.float32).astype(ml_dtypes.bfloat16)).reshape(k // 32, 32, n)
    amax = np.abs(w).max(1)
    byte = np.clip(np.where(amax > 0, np.frexp(amax)[1] - 1 + 127 - 7, 1), 1, 254)
    scaled = (w * np.exp2(127.0 - byte)[:, None, :]).reshape(k, n).astype(np.float32)
    words = np.ascontiguousarray(scaled.reshape(k // 512, 128, 4, n).transpose(0, 1, 3, 2)).astype(ml_dtypes.float8_e4m3fn).view(np.uint8)
    return words, np.ascontiguousarray(byte.astype(np.uint8).reshape(k // 512, 16, n))


def unpack_weight(words, scales):
    g, p, n, _ = words.shape
    vals = np.ascontiguousarray(words).view(ml_dtypes.float8_e4m3fn).astype(np.float64) * np.repeat(np.exp2(scales.astype(np.float64) - 127.0), 8, axis=1)[..., None]
    return vals.transpose(0, 1, 3, 2).reshape(g * 512, n)


K, T, S, N, H = 512, 2048, 512, 128, 512


def setup_inputs():
    n = np.random.standard_normal
    s = mx_kscale(K)[:, None]
    u = mx_kscale(H)
    packed_xT = pack_weight(n((K, T)) * s)
    return {
        "x_words": packed_xT[0],
        "x_scales": packed_xT[1],
        "w1": (n((K, H)) / np.sqrt(K) / s).astype(np.float32),
        "w2": (n((K, H)) / np.sqrt(K) / s).astype(np.float32),
        "f0": (np.random.uniform(0.8, 1.2, (H, S))).astype(np.float32),
        "dr": (np.random.uniform(0.3, 0.8, (H, 1))).astype(np.float32),
        "unit": (np.random.uniform(0.6, 1.4, (H, 1)) * u[:, None]).astype(np.float32),
        "w3": (n((H, N)) / np.sqrt(H) / u[:, None]).astype(np.float32),
        "offs": striped(np.random.permutation(T)[:S]),
        "nb": striped(np.random.permutation(S)),
    }


def reference(x_words, x_scales, w1, w2, f0, dr, unit, w3, offs, nb):
    xq = unpack_weight(x_words, x_scales)[:, unstriped(offs)]
    pw = mxq(f64(w1), 0, "e4m3").T @ xq
    vt = mxq(f64(w2), 0, "e4m3").T @ xq
    volt = 0.3 * np.tanh(vt) + 1.0
    vn = volt[:, unstriped(nb)]
    freq = f64(f0) - (f64(dr) * np.tanh(pw))
    fn = freq[:, unstriped(nb)]
    slip = freq - fn
    flow = (volt * vn) * np.tanh(2.0 * slip)
    pnew = pw + 0.8 * flow
    hid = f64(unit) * (pnew - (1.5 * ((slip) ** 2)))
    return mxq(f64(w3), 0, "e4m3").T @ mxq(hid, 0, "e4m3")

@@ -1,0 +1,226 @@
+from contextlib import ExitStack
+
+import concourse.mybir as mybir
+
+K, T, S, N, H = 512, 2048, 512, 128, 512
+FLOPS = 2 * K * H * S * 2 + 2 * H * N * S
+
+F32 = mybir.dt.float32
+BF16 = mybir.dt.bfloat16
+I32 = mybir.dt.int32
+U32 = mybir.dt.uint32
+U16 = mybir.dt.uint16
+U8 = mybir.dt.uint8
+FP8X4 = mybir.dt.float8_e4m3fn_x4
+ACT = mybir.ActivationFunctionType
+ALU = mybir.AluOpType
+
+P = 128
+PACK = 4
+HALF = S // 2
+LIST_COLS = S // 16
+
+
+def tile_picked_ydroopc_pow_p_kernel(
+    tc, x_words, x_scales, w1, w2, f0, dr, unit, w3, offs, nb, out
+):
+    nc = tc.nc
+    with ExitStack() as ctx:
+        keep = ctx.enter_context(tc.tile_pool(name="keep", bufs=1))
+        psum = ctx.enter_context(tc.psum_pool(name="psum", bufs=1))
+
+        offs_sb = keep.tile([P, LIST_COLS], U16, name="offs_sb")
+        nb_sb = keep.tile([P, LIST_COLS], U16, name="nb_sb")
+        table_words = keep.tile([P, T], I32, name="table_words", align_bytes=64)
+        table_scales = keep.tile([P, T], U8, name="table_scales", align_bytes=64)
+        dr_sb = keep.tile([P, PACK], F32, name="dr_sb")
+        unit_sb = keep.tile([P, PACK], F32, name="unit_sb")
+        w_raw = [[keep.tile([P, PACK, H // 2], F32, name="w%d_raw%d" % (a, c)) for c in range(2)] for a in range(2)]
+        w3_raw = keep.tile([P, PACK, N], F32, name="w3_raw")
+        f0_sb = [keep.tile([P, S], F32, name="f0_%d" % t) for t in range(PACK)]
+
+        def load_weight(a, w, c):
+            rows = w.rearrange("(p j) c -> p j c", j=PACK)
+            nc.sync.dma_start(out=w_raw[a][c][:], in_=rows[:, :, c * (H // 2) : (c + 1) * (H // 2)])
+
+        f0_rows = f0.rearrange("(p t) j -> p t j", t=PACK)
+
+        nc.vector.memset(table_scales[:].bitcast(I32), 0)
+        load_weight(0, w1, 0)
+        for q in range(4):
+            nc.sync.dma_start(
+                out=table_scales[32 * q : 32 * q + 4, :].bitcast(I32),
+                in_=x_scales[0, 4 * q : 4 * q + 4, :].bitcast(I32),
+            )
+        nc.sync.dma_start(out=offs_sb[:], in_=offs)
+        load_weight(0, w1, 1)
+        nc.sync.dma_start(out=table_words[:], in_=x_words[0].rearrange("p c r -> p (c r)").bitcast(I32))
+        nc.sync.dma_start(out=dr_sb[:], in_=dr.rearrange("(p t) o -> p (t o)", t=PACK))
+        nc.sync.dma_start(out=f0_sb[0][:], in_=f0_rows[:, 0, :])
+        nc.sync.dma_start(out=nb_sb[:], in_=nb)
+        nc.sync.dma_start(out=f0_sb[1][:], in_=f0_rows[:, 1, :])
+        load_weight(1, w2, 0)
+        load_weight(1, w2, 1)
+        nc.sync.dma_start(out=f0_sb[2][:], in_=f0_rows[:, 2, :])
+        nc.sync.dma_start(out=f0_sb[3][:], in_=f0_rows[:, 3, :])
+        nc.sync.dma_start(out=unit_sb[:], in_=unit.rearrange("(p t) o -> p (t o)", t=PACK))
+        nc.sync.dma_start(out=w3_raw[:], in_=w3.rearrange("(p j) n -> p j n", j=PACK))
+
+        w_grouped = [keep.tile([P, PACK, P, PACK], BF16, name="w%d_grouped" % a, align_bytes=64) for a in range(2)]
+        w_codes = [keep.tile([P, H], U32, name="w%d_codes" % a, align_bytes=64) for a in range(2)]
+        w_scales = [keep.tile([P, H], U8, name="w%d_scales" % a, align_bytes=64) for a in range(2)]
+
+        def round_weight(a, c, copy):
+            dst = w_grouped[a][:, :, c * (P // 2) : (c + 1) * (P // 2), :].rearrange("p t m j -> p m j t")
+            copy(out=dst, in_=w_raw[a][c][:].rearrange("p j (m t) -> p m j t", t=PACK))
+
+        def quantize_weight(a):
+            nc.vector.quantize_mx(
+                out=w_codes[a][:].bitcast(FP8X4),
+                scales=w_scales[a][:],
+                in_=w_grouped[a][:].rearrange("p t m j -> p (t m j)"),
+            )
+
+        x_codes = keep.tile([P, S], U32, name="x_codes", align_bytes=64)
+        x_bytes = keep.tile([P, S], U8, name="x_bytes", align_bytes=64)
+        nc.vector.tensor_copy(x_bytes[:], table_scales[:].indirect(offs_sb[:]))
+
+        round_weight(0, 0, nc.scalar.copy)
+        round_weight(0, 1, nc.vector.tensor_copy)
+        quantize_weight(0)
+
+        def entries(a_list, cols):
+            return a_list[:, cols.start // 16 : cols.stop // 16]
+
+        halves = [slice(0, HALF), slice(HALF, S)]
+        for cols in halves:
+            nc.vector.tensor_copy(x_codes[:, cols], table_words[:].bitcast(U32).indirect(entries(offs_sb, cols)))
+
+        def product(a, t, bank, cols):
+            w_cols = slice(t * P, (t + 1) * P)
+            nc.tensor.matmul_mx(
+                out=bank[:, cols],
+                lhsT=w_codes[a][:, w_cols].bitcast(FP8X4),
+                lhsT_scale=w_scales[a][:, w_cols],
+                rhs=x_codes[:, cols].bitcast(FP8X4),
+                rhs_scale=x_bytes[:, cols],
+                start=True,
+                stop=True,
+            )
+
+        def rows(name):
+            return [keep.tile([P, S], F32, name="%s%d" % (name, t)) for t in range(PACK)]
+
+        pw = [psum.tile([P, S], F32, name="pw%d" % t) for t in range(PACK)]
+        tanh_pw, neg_freq, neg_fn, neg_slip = rows("tanh_pw"), rows("neg_freq"), rows("neg_fn"), rows("neg_slip")
+        tanh_slip, slip_sq, damped = rows("tanh_slip"), rows("slip_sq"), rows("damped")
+        tanh_vt, vn, both, flow = rows("tanh_vt"), rows("vn"), rows("both"), rows("flow")
+        flow_gain = keep.tile([P, PACK], F32, name="flow_gain")
+        hid = keep.tile([P, PACK, S], BF16, name="hid", align_bytes=64)
+
+        def power_stage(t):
+            product(0, t, pw[t], slice(0, S))
+            nc.scalar.activation(tanh_pw[t][:], pw[t][:], ACT.Tanh)
+            nc.vector.scalar_tensor_tensor(
+                neg_freq[t][:], tanh_pw[t][:], dr_sb[:, t : t + 1], f0_sb[t][:], ALU.mult, ALU.subtract
+            )
+
+        def slip_stage(t):
+            for cols in halves:
+                nc.scalar.activation(neg_fn[t][:, cols], neg_freq[t][:].indirect(entries(nb_sb, cols)), ACT.Copy)
+            nc.vector.tensor_tensor(neg_slip[t][:], neg_freq[t][:], neg_fn[t][:], ALU.subtract)
+
+        def bound_stage(t):
+            nc.scalar.activation(tanh_slip[t][:], neg_slip[t][:], ACT.Tanh, scale=-2.0)
+            nc.scalar.activation(slip_sq[t][:], neg_slip[t][:], ACT.Square)
+            nc.vector.scalar_tensor_tensor(damped[t][:], slip_sq[t][:], -1.5, pw[t][:], ALU.mult, ALU.add)
+
+        def volt_stage(t):
+            vt = psum.tile([P, S], F32, name="vt", bufs=2)
+            product(1, t, vt, slice(0, S))
+            nc.scalar.activation(tanh_vt[t][:], vt[:], ACT.Tanh)
+
+        def neighbour_volts(t, cols):
+            window = tanh_vt[t][:].indirect(entries(nb_sb, cols))
+            nc.scalar.activation(vn[t][:, cols], window, ACT.Copy, bias=1.0, scale=0.3)
+
+        def flow_stage(t, cols):
+            nc.vector.scalar_tensor_tensor(
+                both[t][:, cols], tanh_vt[t][:, cols], 1.0 / 0.3, vn[t][:, cols], ALU.add, ALU.mult
+            )
+            nc.vector.scalar_tensor_tensor(
+                flow[t][:, cols], both[t][:, cols], flow_gain[:, t : t + 1], tanh_slip[t][:, cols], ALU.mult, ALU.mult
+            )
+            nc.vector.scalar_tensor_tensor(
+                hid[:, t, cols], damped[t][:, cols], unit_sb[:, t : t + 1], flow[t][:, cols], ALU.mult, ALU.add
+            )
+
+        w3_grouped = keep.tile([P, N, PACK], BF16, name="w3_grouped", align_bytes=64)
+        w3_codes = keep.tile([P, N], U32, name="w3_codes", align_bytes=64)
+        w3_scales = keep.tile([P, N], U8, name="w3_scales", align_bytes=64)
+
+        def interleave(dst, src, copy):
+            copy(
+                out=dst.rearrange("p (c i) t -> p c t i", i=PACK),
+                in_=src.rearrange("p t (c i) -> p c t i", i=PACK),
+            )
+
+        def feeder_stage(cols):
+            h, width = cols.start, cols.stop - cols.start
+            grouped = keep.tile([P, width, PACK], BF16, name="hid_grouped%d" % h, align_bytes=64)
+            codes = keep.tile([P, width], U32, name="hid_codes%d" % h, align_bytes=64)
+            scales = keep.tile([P, width], U8, name="hid_scales%d" % h, align_bytes=64)
+            interleave(grouped[:], hid[:, :, cols], nc.vector.tensor_copy)
+            nc.vector.quantize_mx(
+                out=codes[:].bitcast(FP8X4), scales=scales[:], in_=grouped[:].rearrange("p c t -> p (c t)")
+            )
+            acc = psum.tile([P, width], F32, name="acc", bufs=2)
+            nc.tensor.matmul_mx(
+                out=acc[:],
+                lhsT=w3_codes[:].bitcast(FP8X4),
+                lhsT_scale=w3_scales[:],
+                rhs=codes[:].bitcast(FP8X4),
+                rhs_scale=scales[:],
+                start=True,
+                stop=True,
+            )
+            result = keep.tile([P, width], F32, name="result%d" % h)
+            nc.scalar.copy(out=result[:], in_=acc[:])
+            nc.sync.dma_start(out=out[:, cols], in_=result[:])
+
+        power_stage(0)
+        power_stage(1)
+        slip_stage(0)
+        for c in range(2):
+            round_weight(1, c, nc.vector.tensor_copy)
+        quantize_weight(1)
+        power_stage(2)
+        bound_stage(0)
+        slip_stage(1)
+        nc.vector.tensor_scalar(flow_gain[:], unit_sb[:], 0.8 * 0.3, None, ALU.mult)
+        interleave(w3_grouped[:], w3_raw[:], nc.vector.tensor_copy)
+        nc.vector.quantize_mx(
+            out=w3_codes[:].bitcast(FP8X4), scales=w3_scales[:], in_=w3_grouped[:].rearrange("p n j -> p (n j)")
+        )
+        whole = slice(0, S)
+        power_stage(3)
+        volt_stage(0)
+        bound_stage(1)
+        for cols in halves:
+            neighbour_volts(0, cols)
+        flow_stage(0, whole)
+        slip_stage(2)
+        volt_stage(1)
+        bound_stage(2)
+        for cols in halves:
+            neighbour_volts(1, cols)
+        flow_stage(1, whole)
+        slip_stage(3)
+        volt_stage(2)
+        volt_stage(3)
+        bound_stage(3)
+        for cols in (slice(0, 256), slice(256, 384), slice(384, 512)):
+            for t in (2, 3):
+                neighbour_volts(t, cols)
+                flow_stage(t, cols)
+            feeder_stage(cols)

@@ -17,8 +17,10 @@ ALU = mybir.AluOpType
 
 P = 128
 PACK = 4
-HALF = S // 2
-LIST_COLS = S // 16
+GROUP = 16
+WHOLE = slice(0, S)
+HALVES = (slice(0, S // 2), slice(S // 2, S))
+PIECES = (slice(0, 256), slice(256, 384), slice(384, 512))
 
 
 def tile_picked_ydroopc_pow_p_kernel(
@@ -29,198 +31,170 @@ def tile_picked_ydroopc_pow_p_kernel(
         keep = ctx.enter_context(tc.tile_pool(name="keep", bufs=1))
         psum = ctx.enter_context(tc.psum_pool(name="psum", bufs=1))
 
-        offs_sb = keep.tile([P, LIST_COLS], U16, name="offs_sb")
-        nb_sb = keep.tile([P, LIST_COLS], U16, name="nb_sb")
+        offs_sb = keep.tile([P, S // GROUP], U16, name="offs_sb")
+        nb_sb = keep.tile([P, S // GROUP], U16, name="nb_sb")
         table_words = keep.tile([P, T], I32, name="table_words", align_bytes=64)
         table_scales = keep.tile([P, T], U8, name="table_scales", align_bytes=64)
         dr_sb = keep.tile([P, PACK], F32, name="dr_sb")
         unit_sb = keep.tile([P, PACK], F32, name="unit_sb")
-        w_raw = [[keep.tile([P, PACK, H // 2], F32, name="w%d_raw%d" % (a, c)) for c in range(2)] for a in range(2)]
+        w_raw = [keep.tile([P, PACK, H], F32, name="w%d_raw" % a) for a in (1, 2)]
         w3_raw = keep.tile([P, PACK, N], F32, name="w3_raw")
         f0_sb = [keep.tile([P, S], F32, name="f0_%d" % t) for t in range(PACK)]
-
-        def load_weight(a, w, c):
-            rows = w.rearrange("(p j) c -> p j c", j=PACK)
-            nc.sync.dma_start(out=w_raw[a][c][:], in_=rows[:, :, c * (H // 2) : (c + 1) * (H // 2)])
-
         f0_rows = f0.rearrange("(p t) j -> p t j", t=PACK)
 
         nc.vector.memset(table_scales[:].bitcast(I32), 0)
-        load_weight(0, w1, 0)
+        nc.sync.dma_start(out=offs_sb[:], in_=offs)
+        nc.sync.dma_start(out=dr_sb[:], in_=dr.rearrange("(p t) o -> p (t o)", t=PACK))
+        nc.sync.dma_start(out=w_raw[0][:], in_=w1.rearrange("(p j) c -> p j c", j=PACK))
+        nc.sync.dma_start(out=unit_sb[:], in_=unit.rearrange("(p t) o -> p (t o)", t=PACK))
+        nc.sync.dma_start(out=nb_sb[:], in_=nb)
         for q in range(4):
             nc.sync.dma_start(
                 out=table_scales[32 * q : 32 * q + 4, :].bitcast(I32),
                 in_=x_scales[0, 4 * q : 4 * q + 4, :].bitcast(I32),
             )
-        nc.sync.dma_start(out=offs_sb[:], in_=offs)
-        load_weight(0, w1, 1)
         nc.sync.dma_start(out=table_words[:], in_=x_words[0].rearrange("p c r -> p (c r)").bitcast(I32))
-        nc.sync.dma_start(out=dr_sb[:], in_=dr.rearrange("(p t) o -> p (t o)", t=PACK))
         nc.sync.dma_start(out=f0_sb[0][:], in_=f0_rows[:, 0, :])
-        nc.sync.dma_start(out=nb_sb[:], in_=nb)
         nc.sync.dma_start(out=f0_sb[1][:], in_=f0_rows[:, 1, :])
-        load_weight(1, w2, 0)
-        load_weight(1, w2, 1)
+        nc.sync.dma_start(out=w3_raw[:], in_=w3.rearrange("(p j) n -> p j n", j=PACK))
+        nc.sync.dma_start(out=w_raw[1][:], in_=w2.rearrange("(p j) c -> p j c", j=PACK))
         nc.sync.dma_start(out=f0_sb[2][:], in_=f0_rows[:, 2, :])
         nc.sync.dma_start(out=f0_sb[3][:], in_=f0_rows[:, 3, :])
-        nc.sync.dma_start(out=unit_sb[:], in_=unit.rearrange("(p t) o -> p (t o)", t=PACK))
-        nc.sync.dma_start(out=w3_raw[:], in_=w3.rearrange("(p j) n -> p j n", j=PACK))
 
-        w_grouped = [keep.tile([P, PACK, P, PACK], BF16, name="w%d_grouped" % a, align_bytes=64) for a in range(2)]
-        w_codes = [keep.tile([P, H], U32, name="w%d_codes" % a, align_bytes=64) for a in range(2)]
-        w_scales = [keep.tile([P, H], U8, name="w%d_scales" % a, align_bytes=64) for a in range(2)]
+        def quantize(name, grouped, width):
+            codes = keep.tile([P, width], U32, name=name + "_codes", align_bytes=64)
+            scales = keep.tile([P, width], U8, name=name + "_scales", align_bytes=64)
+            nc.vector.quantize_mx(out=codes[:].bitcast(FP8X4), scales=scales[:], in_=grouped)
+            return codes, scales
 
-        def round_weight(a, c, copy):
-            dst = w_grouped[a][:, :, c * (P // 2) : (c + 1) * (P // 2), :].rearrange("p t m j -> p m j t")
-            copy(out=dst, in_=w_raw[a][c][:].rearrange("p j (m t) -> p m j t", t=PACK))
-
-        def quantize_weight(a):
-            nc.vector.quantize_mx(
-                out=w_codes[a][:].bitcast(FP8X4),
-                scales=w_scales[a][:],
-                in_=w_grouped[a][:].rearrange("p t m j -> p (t m j)"),
-            )
-
-        x_codes = keep.tile([P, S], U32, name="x_codes", align_bytes=64)
-        x_bytes = keep.tile([P, S], U8, name="x_bytes", align_bytes=64)
-        nc.vector.tensor_copy(x_bytes[:], table_scales[:].indirect(offs_sb[:]))
-
-        round_weight(0, 0, nc.scalar.copy)
-        round_weight(0, 1, nc.vector.tensor_copy)
-        quantize_weight(0)
+        def dealt_weight(name, raw, copies):
+            grouped = keep.tile([P, PACK, P, PACK], BF16, name=name + "_grouped", align_bytes=64)
+            share = P // len(copies)
+            for c, copy in enumerate(copies):
+                copy(
+                    out=grouped[:, :, c * share : (c + 1) * share, :].rearrange("p t m j -> p m j t"),
+                    in_=raw[:, :, PACK * c * share : PACK * (c + 1) * share].rearrange("p j (m t) -> p m j t", t=PACK),
+                )
+            return grouped[:].rearrange("p t m j -> p (t m j)")
 
         def entries(a_list, cols):
-            return a_list[:, cols.start // 16 : cols.stop // 16]
+            return a_list[:, cols.start // GROUP : cols.stop // GROUP]
 
-        halves = [slice(0, HALF), slice(HALF, S)]
-        for cols in halves:
-            nc.vector.tensor_copy(x_codes[:, cols], table_words[:].bitcast(U32).indirect(entries(offs_sb, cols)))
+        def by_fours(grouped):
+            return grouped.rearrange("p (c i) t -> p c t i", i=PACK)
 
-        def product(a, t, bank, cols):
-            w_cols = slice(t * P, (t + 1) * P)
+        def rows_by_fours(rows):
+            return rows.rearrange("p t (c i) -> p c t i", i=PACK)
+
+        def multiply(acc, lhs, lhs_cols, rhs, rhs_cols):
             nc.tensor.matmul_mx(
-                out=bank[:, cols],
-                lhsT=w_codes[a][:, w_cols].bitcast(FP8X4),
-                lhsT_scale=w_scales[a][:, w_cols],
-                rhs=x_codes[:, cols].bitcast(FP8X4),
-                rhs_scale=x_bytes[:, cols],
+                out=acc,
+                lhsT=lhs[0][:, lhs_cols].bitcast(FP8X4),
+                lhsT_scale=lhs[1][:, lhs_cols],
+                rhs=rhs[0][:, rhs_cols].bitcast(FP8X4),
+                rhs_scale=rhs[1][:, rhs_cols],
                 start=True,
                 stop=True,
             )
+
+        w1_dealt = dealt_weight("w1", w_raw[0], (nc.scalar.copy, nc.vector.tensor_copy))
+        x_codes = keep.tile([P, S], U32, name="x_codes", align_bytes=64)
+        x_bytes = keep.tile([P, S], U8, name="x_bytes", align_bytes=64)
+        x_mx = (x_codes, x_bytes)
+        nc.vector.tensor_copy(x_bytes[:], table_scales[:].indirect(offs_sb[:]))
+        w1_mx = quantize("w1", w1_dealt, H)
+        for cols in HALVES:
+            nc.vector.tensor_copy(x_codes[:, cols], table_words[:].bitcast(U32).indirect(entries(offs_sb, cols)))
+
+        slip_gain = keep.tile([P, PACK], F32, name="slip_gain")
+        flow_gain = keep.tile([P, PACK], F32, name="flow_gain")
+        nc.vector.tensor_scalar(slip_gain[:], unit_sb[:], -1.5, None, ALU.mult)
+        nc.vector.tensor_scalar(flow_gain[:], unit_sb[:], 0.8 * 0.3, None, ALU.mult)
 
         def rows(name):
             return [keep.tile([P, S], F32, name="%s%d" % (name, t)) for t in range(PACK)]
 
-        pw = [psum.tile([P, S], F32, name="pw%d" % t) for t in range(PACK)]
         tanh_pw, neg_freq, neg_fn, neg_slip = rows("tanh_pw"), rows("neg_freq"), rows("neg_fn"), rows("neg_slip")
-        tanh_slip, slip_sq, damped = rows("tanh_slip"), rows("slip_sq"), rows("damped")
-        tanh_vt, vn, both, flow = rows("tanh_vt"), rows("vn"), rows("both"), rows("flow")
-        flow_gain = keep.tile([P, PACK], F32, name="flow_gain")
-        hid = keep.tile([P, PACK, S], BF16, name="hid", align_bytes=64)
+        tanh_slip, damping, tanh_vt, own, vn = rows("tanh_slip"), rows("damping"), rows("tanh_vt"), rows("own"), rows("vn")
+        damped = keep.tile([P, PACK, S], F32, name="damped")
+        pw = {}
 
-        def power_stage(t):
-            product(0, t, pw[t], slice(0, S))
-            nc.scalar.activation(tanh_pw[t][:], pw[t][:], ACT.Tanh)
-            nc.vector.scalar_tensor_tensor(
-                neg_freq[t][:], tanh_pw[t][:], dr_sb[:, t : t + 1], f0_sb[t][:], ALU.mult, ALU.subtract
-            )
+        def power(t):
+            pw[t] = []
+            for cols in HALVES if t == 0 else (WHOLE,):
+                width = cols.stop - cols.start
+                if t == 0:
+                    bank = psum.tile([P, width], F32, name="acc", bufs=2)
+                else:
+                    bank = psum.tile([P, width], F32, name="pw%d" % t)
+                pw[t].append((cols, bank))
+                multiply(bank[:], w1_mx, slice(t * P, (t + 1) * P), x_mx, cols)
+                nc.scalar.activation(tanh_pw[t][:, cols], bank[:], ACT.Tanh)
+                nc.vector.scalar_tensor_tensor(
+                    neg_freq[t][:, cols], tanh_pw[t][:, cols], dr_sb[:, t : t + 1], f0_sb[t][:, cols],
+                    ALU.mult, ALU.subtract,
+                )
 
-        def slip_stage(t):
-            for cols in halves:
+        def neighbour_freqs(t):
+            for cols in HALVES:
                 nc.scalar.activation(neg_fn[t][:, cols], neg_freq[t][:].indirect(entries(nb_sb, cols)), ACT.Copy)
+
+        def slip(t):
             nc.vector.tensor_tensor(neg_slip[t][:], neg_freq[t][:], neg_fn[t][:], ALU.subtract)
 
-        def bound_stage(t):
+        def slip_terms(t):
             nc.scalar.activation(tanh_slip[t][:], neg_slip[t][:], ACT.Tanh, scale=-2.0)
-            nc.scalar.activation(slip_sq[t][:], neg_slip[t][:], ACT.Square)
-            nc.vector.scalar_tensor_tensor(damped[t][:], slip_sq[t][:], -1.5, pw[t][:], ALU.mult, ALU.add)
+            nc.vector.scalar_tensor_tensor(
+                damping[t][:], neg_slip[t][:], slip_gain[:, t : t + 1], neg_slip[t][:], ALU.mult, ALU.mult
+            )
+            for cols, bank in pw[t]:
+                nc.vector.scalar_tensor_tensor(
+                    damped[:, t, cols], bank[:], unit_sb[:, t : t + 1], damping[t][:, cols], ALU.mult, ALU.add
+                )
 
-        def volt_stage(t):
-            vt = psum.tile([P, S], F32, name="vt", bufs=2)
-            product(1, t, vt, slice(0, S))
+        def voltage(t, w2_mx):
+            vt = psum.tile([P, S], F32, name="vt", bufs=3)
+            multiply(vt[:], w2_mx, slice(t * P, (t + 1) * P), x_mx, WHOLE)
             nc.scalar.activation(tanh_vt[t][:], vt[:], ACT.Tanh)
+            nc.vector.scalar_tensor_tensor(own[t][:], tanh_vt[t][:], 1.0 / 0.3, tanh_slip[t][:], ALU.add, ALU.mult)
 
-        def neighbour_volts(t, cols):
-            window = tanh_vt[t][:].indirect(entries(nb_sb, cols))
-            nc.scalar.activation(vn[t][:, cols], window, ACT.Copy, bias=1.0, scale=0.3)
-
-        def flow_stage(t, cols):
-            nc.vector.scalar_tensor_tensor(
-                both[t][:, cols], tanh_vt[t][:, cols], 1.0 / 0.3, vn[t][:, cols], ALU.add, ALU.mult
+        def feeders(cols, w3_mx):
+            width = cols.stop - cols.start
+            name = "hid%d" % cols.start
+            flow = keep.tile([P, PACK, width], F32, name=name + "_flow")
+            for t in range(PACK):
+                window = tanh_vt[t][:].indirect(entries(nb_sb, cols))
+                nc.scalar.activation(vn[t][:, cols], window, ACT.Copy, bias=1.0, scale=0.3)
+                nc.vector.scalar_tensor_tensor(
+                    flow[:, t, :], vn[t][:, cols], flow_gain[:, t : t + 1], own[t][:, cols], ALU.mult, ALU.mult
+                )
+            grouped = keep.tile([P, width, PACK], BF16, name=name + "_grouped", align_bytes=64)
+            nc.vector.tensor_tensor(
+                by_fours(grouped[:]), rows_by_fours(damped[:, :, cols]), rows_by_fours(flow[:]), ALU.add
             )
-            nc.vector.scalar_tensor_tensor(
-                flow[t][:, cols], both[t][:, cols], flow_gain[:, t : t + 1], tanh_slip[t][:, cols], ALU.mult, ALU.mult
-            )
-            nc.vector.scalar_tensor_tensor(
-                hid[:, t, cols], damped[t][:, cols], unit_sb[:, t : t + 1], flow[t][:, cols], ALU.mult, ALU.add
-            )
-
-        w3_grouped = keep.tile([P, N, PACK], BF16, name="w3_grouped", align_bytes=64)
-        w3_codes = keep.tile([P, N], U32, name="w3_codes", align_bytes=64)
-        w3_scales = keep.tile([P, N], U8, name="w3_scales", align_bytes=64)
-
-        def interleave(dst, src, copy):
-            copy(
-                out=dst.rearrange("p (c i) t -> p c t i", i=PACK),
-                in_=src.rearrange("p t (c i) -> p c t i", i=PACK),
-            )
-
-        def feeder_stage(cols):
-            h, width = cols.start, cols.stop - cols.start
-            grouped = keep.tile([P, width, PACK], BF16, name="hid_grouped%d" % h, align_bytes=64)
-            codes = keep.tile([P, width], U32, name="hid_codes%d" % h, align_bytes=64)
-            scales = keep.tile([P, width], U8, name="hid_scales%d" % h, align_bytes=64)
-            interleave(grouped[:], hid[:, :, cols], nc.vector.tensor_copy)
-            nc.vector.quantize_mx(
-                out=codes[:].bitcast(FP8X4), scales=scales[:], in_=grouped[:].rearrange("p c t -> p (c t)")
-            )
+            hid_mx = quantize(name, grouped[:].rearrange("p c t -> p (c t)"), width)
             acc = psum.tile([P, width], F32, name="acc", bufs=2)
-            nc.tensor.matmul_mx(
-                out=acc[:],
-                lhsT=w3_codes[:].bitcast(FP8X4),
-                lhsT_scale=w3_scales[:],
-                rhs=codes[:].bitcast(FP8X4),
-                rhs_scale=scales[:],
-                start=True,
-                stop=True,
-            )
-            result = keep.tile([P, width], F32, name="result%d" % h)
+            multiply(acc[:], w3_mx, slice(0, N), hid_mx, slice(0, width))
+            result = keep.tile([P, width], F32, name=name + "_result")
             nc.scalar.copy(out=result[:], in_=acc[:])
             nc.sync.dma_start(out=out[:, cols], in_=result[:])
 
-        power_stage(0)
-        power_stage(1)
-        slip_stage(0)
-        for c in range(2):
-            round_weight(1, c, nc.vector.tensor_copy)
-        quantize_weight(1)
-        power_stage(2)
-        bound_stage(0)
-        slip_stage(1)
-        nc.vector.tensor_scalar(flow_gain[:], unit_sb[:], 0.8 * 0.3, None, ALU.mult)
-        interleave(w3_grouped[:], w3_raw[:], nc.vector.tensor_copy)
-        nc.vector.quantize_mx(
-            out=w3_codes[:].bitcast(FP8X4), scales=w3_scales[:], in_=w3_grouped[:].rearrange("p n j -> p (n j)")
-        )
-        whole = slice(0, S)
-        power_stage(3)
-        volt_stage(0)
-        bound_stage(1)
-        for cols in halves:
-            neighbour_volts(0, cols)
-        flow_stage(0, whole)
-        slip_stage(2)
-        volt_stage(1)
-        bound_stage(2)
-        for cols in halves:
-            neighbour_volts(1, cols)
-        flow_stage(1, whole)
-        slip_stage(3)
-        volt_stage(2)
-        volt_stage(3)
-        bound_stage(3)
-        for cols in (slice(0, 256), slice(256, 384), slice(384, 512)):
-            for t in (2, 3):
-                neighbour_volts(t, cols)
-                flow_stage(t, cols)
-            feeder_stage(cols)
+        power(0)
+        power(1)
+        neighbour_freqs(0)
+        slip(0)
+        w2_mx = quantize("w2", dealt_weight("w2", w_raw[1], (nc.vector.tensor_copy,)), H)
+        for t in range(1, PACK):
+            if t + 1 < PACK:
+                power(t + 1)
+            neighbour_freqs(t)
+            slip_terms(t - 1)
+            slip(t)
+        slip_terms(PACK - 1)
+        w3_grouped = keep.tile([P, N, PACK], BF16, name="w3_grouped", align_bytes=64)
+        nc.vector.tensor_copy(out=by_fours(w3_grouped[:]), in_=rows_by_fours(w3_raw[:]))
+        w3_mx = quantize("w3", w3_grouped[:].rearrange("p n j -> p (n j)"), N)
+        for t in range(PACK):
+            voltage(t, w2_mx)
+        for cols in PIECES:
+            feeders(cols, w3_mx)

@@ -20,7 +20,7 @@ PACK = 4
 GROUP = 16
 WHOLE = slice(0, S)
 HALVES = (slice(0, S // 2), slice(S // 2, S))
-PIECES = (slice(0, 256), slice(256, 384), slice(384, 512))
+PIECES = (slice(0, 128), slice(128, 384), slice(384, 512))
 
 
 def tile_picked_ydroopc_pow_p_kernel(
@@ -34,7 +34,7 @@ def tile_picked_ydroopc_pow_p_kernel(
         offs_sb = keep.tile([P, S // GROUP], U16, name="offs_sb")
         nb_sb = keep.tile([P, S // GROUP], U16, name="nb_sb")
         table_words = keep.tile([P, T], I32, name="table_words", align_bytes=64)
-        table_scales = keep.tile([P, T], U8, name="table_scales", align_bytes=64)
+        table_scales = keep.tile([P, T], U8, name="table_scales", tag="table_scales", align_bytes=64)
         dr_sb = keep.tile([P, PACK], F32, name="dr_sb")
         unit_sb = keep.tile([P, PACK], F32, name="unit_sb")
         w_raw = [keep.tile([P, PACK, H], F32, name="w%d_raw" % a) for a in (1, 2)]
@@ -44,10 +44,9 @@ def tile_picked_ydroopc_pow_p_kernel(
 
         nc.vector.memset(table_scales[:].bitcast(I32), 0)
         nc.sync.dma_start(out=offs_sb[:], in_=offs)
-        nc.sync.dma_start(out=dr_sb[:], in_=dr.rearrange("(p t) o -> p (t o)", t=PACK))
         nc.sync.dma_start(out=w_raw[0][:], in_=w1.rearrange("(p j) c -> p j c", j=PACK))
+        nc.sync.dma_start(out=dr_sb[:], in_=dr.rearrange("(p t) o -> p (t o)", t=PACK))
         nc.sync.dma_start(out=unit_sb[:], in_=unit.rearrange("(p t) o -> p (t o)", t=PACK))
-        nc.sync.dma_start(out=nb_sb[:], in_=nb)
         for q in range(4):
             nc.sync.dma_start(
                 out=table_scales[32 * q : 32 * q + 4, :].bitcast(I32),
@@ -55,15 +54,16 @@ def tile_picked_ydroopc_pow_p_kernel(
             )
         nc.sync.dma_start(out=table_words[:], in_=x_words[0].rearrange("p c r -> p (c r)").bitcast(I32))
         nc.sync.dma_start(out=f0_sb[0][:], in_=f0_rows[:, 0, :])
-        nc.sync.dma_start(out=f0_sb[1][:], in_=f0_rows[:, 1, :])
+        nc.sync.dma_start(out=nb_sb[:], in_=nb)
         nc.sync.dma_start(out=w3_raw[:], in_=w3.rearrange("(p j) n -> p j n", j=PACK))
-        nc.sync.dma_start(out=w_raw[1][:], in_=w2.rearrange("(p j) c -> p j c", j=PACK))
+        nc.sync.dma_start(out=f0_sb[1][:], in_=f0_rows[:, 1, :])
         nc.sync.dma_start(out=f0_sb[2][:], in_=f0_rows[:, 2, :])
+        nc.sync.dma_start(out=w_raw[1][:], in_=w2.rearrange("(p j) c -> p j c", j=PACK))
         nc.sync.dma_start(out=f0_sb[3][:], in_=f0_rows[:, 3, :])
 
-        def quantize(name, grouped, width):
+        def quantize(name, grouped, width, scales_tag=None):
             codes = keep.tile([P, width], U32, name=name + "_codes", align_bytes=64)
-            scales = keep.tile([P, width], U8, name=name + "_scales", align_bytes=64)
+            scales = keep.tile([P, width], U8, name=name + "_scales", tag=scales_tag or name + "_scales", align_bytes=64)
             nc.vector.quantize_mx(out=codes[:].bitcast(FP8X4), scales=scales[:], in_=grouped)
             return codes, scales
 
@@ -102,14 +102,12 @@ def tile_picked_ydroopc_pow_p_kernel(
         x_bytes = keep.tile([P, S], U8, name="x_bytes", align_bytes=64)
         x_mx = (x_codes, x_bytes)
         nc.vector.tensor_copy(x_bytes[:], table_scales[:].indirect(offs_sb[:]))
-        w1_mx = quantize("w1", w1_dealt, H)
+        w1_mx = quantize("w1", w1_dealt, H, scales_tag="table_scales")
         for cols in HALVES:
             nc.vector.tensor_copy(x_codes[:, cols], table_words[:].bitcast(U32).indirect(entries(offs_sb, cols)))
 
         slip_gain = keep.tile([P, PACK], F32, name="slip_gain")
-        flow_gain = keep.tile([P, PACK], F32, name="flow_gain")
         nc.vector.tensor_scalar(slip_gain[:], unit_sb[:], -1.5, None, ALU.mult)
-        nc.vector.tensor_scalar(flow_gain[:], unit_sb[:], 0.8 * 0.3, None, ALU.mult)
 
         def rows(name):
             return [keep.tile([P, S], F32, name="%s%d" % (name, t)) for t in range(PACK)]
@@ -137,7 +135,11 @@ def tile_picked_ydroopc_pow_p_kernel(
 
         def neighbour_freqs(t):
             for cols in HALVES:
-                nc.scalar.activation(neg_fn[t][:, cols], neg_freq[t][:].indirect(entries(nb_sb, cols)), ACT.Copy)
+                window = neg_freq[t][:].indirect(entries(nb_sb, cols))
+                if t == 0 and cols.start == 0:
+                    nc.vector.tensor_copy(neg_fn[t][:, cols], window)
+                else:
+                    nc.scalar.activation(neg_fn[t][:, cols], window, ACT.Copy)
 
         def slip(t):
             nc.vector.tensor_tensor(neg_slip[t][:], neg_freq[t][:], neg_fn[t][:], ALU.subtract)
@@ -164,9 +166,9 @@ def tile_picked_ydroopc_pow_p_kernel(
             flow = keep.tile([P, PACK, width], F32, name=name + "_flow")
             for t in range(PACK):
                 window = tanh_vt[t][:].indirect(entries(nb_sb, cols))
-                nc.scalar.activation(vn[t][:, cols], window, ACT.Copy, bias=1.0, scale=0.3)
+                nc.scalar.activation(vn[t][:, cols], window, ACT.Copy, bias=0.8 * 0.3, scale=0.8 * 0.3 * 0.3)
                 nc.vector.scalar_tensor_tensor(
-                    flow[:, t, :], vn[t][:, cols], flow_gain[:, t : t + 1], own[t][:, cols], ALU.mult, ALU.mult
+                    flow[:, t, :], vn[t][:, cols], unit_sb[:, t : t + 1], own[t][:, cols], ALU.mult, ALU.mult
                 )
             grouped = keep.tile([P, width, PACK], BF16, name=name + "_grouped", align_bytes=64)
             nc.vector.tensor_tensor(
@@ -177,7 +179,7 @@ def tile_picked_ydroopc_pow_p_kernel(
             multiply(acc[:], w3_mx, slice(0, N), hid_mx, slice(0, width))
             result = keep.tile([P, width], F32, name=name + "_result")
             nc.scalar.copy(out=result[:], in_=acc[:])
-            nc.sync.dma_start(out=out[:, cols], in_=result[:])
+            nc.scalar.dma_start(out=out[:, cols], in_=result[:])
 
         power(0)
         power(1)

from contextlib import ExitStack

import concourse.mybir as mybir

K, T, S, N, H = 512, 2048, 512, 128, 512
FLOPS = 2 * K * H * S * 2 + 2 * H * N * S

F32 = mybir.dt.float32
BF16 = mybir.dt.bfloat16
I32 = mybir.dt.int32
U32 = mybir.dt.uint32
U16 = mybir.dt.uint16
U8 = mybir.dt.uint8
FP8X4 = mybir.dt.float8_e4m3fn_x4
ACT = mybir.ActivationFunctionType
ALU = mybir.AluOpType

P = 128
PACK = 4
GROUP = 16
WHOLE = slice(0, S)
HALVES = (slice(0, S // 2), slice(S // 2, S))
PIECES = (slice(0, 128), slice(128, 384), slice(384, 512))


def tile_picked_ydroopc_pow_p_kernel(
    tc, x_words, x_scales, w1, w2, f0, dr, unit, w3, offs, nb, out
):
    nc = tc.nc
    with ExitStack() as ctx:
        keep = ctx.enter_context(tc.tile_pool(name="keep", bufs=1))
        psum = ctx.enter_context(tc.psum_pool(name="psum", bufs=1))

        offs_sb = keep.tile([P, S // GROUP], U16, name="offs_sb")
        nb_sb = keep.tile([P, S // GROUP], U16, name="nb_sb")
        table_words = keep.tile([P, T], I32, name="table_words", align_bytes=64)
        table_scales = keep.tile([P, T], U8, name="table_scales", tag="table_scales", align_bytes=64)
        dr_sb = keep.tile([P, PACK], F32, name="dr_sb")
        unit_sb = keep.tile([P, PACK], F32, name="unit_sb")
        w_raw = [keep.tile([P, PACK, H], F32, name="w%d_raw" % a) for a in (1, 2)]
        w3_raw = keep.tile([P, PACK, N], F32, name="w3_raw")
        f0_sb = [keep.tile([P, S], F32, name="f0_%d" % t) for t in range(PACK)]
        f0_rows = f0.rearrange("(p t) j -> p t j", t=PACK)

        nc.vector.memset(table_scales[:].bitcast(I32), 0)
        nc.sync.dma_start(out=offs_sb[:], in_=offs)
        nc.sync.dma_start(out=w_raw[0][:], in_=w1.rearrange("(p j) c -> p j c", j=PACK))
        nc.sync.dma_start(out=dr_sb[:], in_=dr.rearrange("(p t) o -> p (t o)", t=PACK))
        nc.sync.dma_start(out=unit_sb[:], in_=unit.rearrange("(p t) o -> p (t o)", t=PACK))
        for q in range(4):
            nc.sync.dma_start(
                out=table_scales[32 * q : 32 * q + 4, :].bitcast(I32),
                in_=x_scales[0, 4 * q : 4 * q + 4, :].bitcast(I32),
            )
        nc.sync.dma_start(out=table_words[:], in_=x_words[0].rearrange("p c r -> p (c r)").bitcast(I32))
        nc.sync.dma_start(out=f0_sb[0][:], in_=f0_rows[:, 0, :])
        nc.sync.dma_start(out=nb_sb[:], in_=nb)
        nc.sync.dma_start(out=w3_raw[:], in_=w3.rearrange("(p j) n -> p j n", j=PACK))
        nc.sync.dma_start(out=f0_sb[1][:], in_=f0_rows[:, 1, :])
        nc.sync.dma_start(out=f0_sb[2][:], in_=f0_rows[:, 2, :])
        nc.sync.dma_start(out=w_raw[1][:], in_=w2.rearrange("(p j) c -> p j c", j=PACK))
        nc.sync.dma_start(out=f0_sb[3][:], in_=f0_rows[:, 3, :])

        def quantize(name, grouped, width, scales_tag=None):
            codes = keep.tile([P, width], U32, name=name + "_codes", align_bytes=64)
            scales = keep.tile([P, width], U8, name=name + "_scales", tag=scales_tag or name + "_scales", align_bytes=64)
            nc.vector.quantize_mx(out=codes[:].bitcast(FP8X4), scales=scales[:], in_=grouped)
            return codes, scales

        def dealt_weight(name, raw, copies):
            grouped = keep.tile([P, PACK, P, PACK], BF16, name=name + "_grouped", align_bytes=64)
            share = P // len(copies)
            for c, copy in enumerate(copies):
                copy(
                    out=grouped[:, :, c * share : (c + 1) * share, :].rearrange("p t m j -> p m j t"),
                    in_=raw[:, :, PACK * c * share : PACK * (c + 1) * share].rearrange("p j (m t) -> p m j t", t=PACK),
                )
            return grouped[:].rearrange("p t m j -> p (t m j)")

        def entries(a_list, cols):
            return a_list[:, cols.start // GROUP : cols.stop // GROUP]

        def by_fours(grouped):
            return grouped.rearrange("p (c i) t -> p c t i", i=PACK)

        def rows_by_fours(rows):
            return rows.rearrange("p t (c i) -> p c t i", i=PACK)

        def multiply(acc, lhs, lhs_cols, rhs, rhs_cols):
            nc.tensor.matmul_mx(
                out=acc,
                lhsT=lhs[0][:, lhs_cols].bitcast(FP8X4),
                lhsT_scale=lhs[1][:, lhs_cols],
                rhs=rhs[0][:, rhs_cols].bitcast(FP8X4),
                rhs_scale=rhs[1][:, rhs_cols],
                start=True,
                stop=True,
            )

        w1_dealt = dealt_weight("w1", w_raw[0], (nc.scalar.copy, nc.vector.tensor_copy))
        x_codes = keep.tile([P, S], U32, name="x_codes", align_bytes=64)
        x_bytes = keep.tile([P, S], U8, name="x_bytes", align_bytes=64)
        x_mx = (x_codes, x_bytes)
        nc.vector.tensor_copy(x_bytes[:], table_scales[:].indirect(offs_sb[:]))
        w1_mx = quantize("w1", w1_dealt, H, scales_tag="table_scales")
        for cols in HALVES:
            nc.vector.tensor_copy(x_codes[:, cols], table_words[:].bitcast(U32).indirect(entries(offs_sb, cols)))

        slip_gain = keep.tile([P, PACK], F32, name="slip_gain")
        nc.vector.tensor_scalar(slip_gain[:], unit_sb[:], -1.5, None, ALU.mult)

        def rows(name):
            return [keep.tile([P, S], F32, name="%s%d" % (name, t)) for t in range(PACK)]

        tanh_pw, neg_freq, neg_fn, neg_slip = rows("tanh_pw"), rows("neg_freq"), rows("neg_fn"), rows("neg_slip")
        tanh_slip, damping, tanh_vt, own, vn = rows("tanh_slip"), rows("damping"), rows("tanh_vt"), rows("own"), rows("vn")
        damped = keep.tile([P, PACK, S], F32, name="damped")
        pw = {}

        def power(t):
            pw[t] = []
            for cols in HALVES if t == 0 else (WHOLE,):
                width = cols.stop - cols.start
                if t == 0:
                    bank = psum.tile([P, width], F32, name="acc", bufs=2)
                else:
                    bank = psum.tile([P, width], F32, name="pw%d" % t)
                pw[t].append((cols, bank))
                multiply(bank[:], w1_mx, slice(t * P, (t + 1) * P), x_mx, cols)
                nc.scalar.activation(tanh_pw[t][:, cols], bank[:], ACT.Tanh)
                nc.vector.scalar_tensor_tensor(
                    neg_freq[t][:, cols], tanh_pw[t][:, cols], dr_sb[:, t : t + 1], f0_sb[t][:, cols],
                    ALU.mult, ALU.subtract,
                )

        def neighbour_freqs(t):
            for cols in HALVES:
                window = neg_freq[t][:].indirect(entries(nb_sb, cols))
                if t == 0 and cols.start == 0:
                    nc.vector.tensor_copy(neg_fn[t][:, cols], window)
                else:
                    nc.scalar.activation(neg_fn[t][:, cols], window, ACT.Copy)

        def slip(t):
            nc.vector.tensor_tensor(neg_slip[t][:], neg_freq[t][:], neg_fn[t][:], ALU.subtract)

        def slip_terms(t):
            nc.scalar.activation(tanh_slip[t][:], neg_slip[t][:], ACT.Tanh, scale=-2.0)
            nc.vector.scalar_tensor_tensor(
                damping[t][:], neg_slip[t][:], slip_gain[:, t : t + 1], neg_slip[t][:], ALU.mult, ALU.mult
            )
            for cols, bank in pw[t]:
                nc.vector.scalar_tensor_tensor(
                    damped[:, t, cols], bank[:], unit_sb[:, t : t + 1], damping[t][:, cols], ALU.mult, ALU.add
                )

        def voltage(t, w2_mx):
            vt = psum.tile([P, S], F32, name="vt", bufs=3)
            multiply(vt[:], w2_mx, slice(t * P, (t + 1) * P), x_mx, WHOLE)
            nc.scalar.activation(tanh_vt[t][:], vt[:], ACT.Tanh)
            nc.vector.scalar_tensor_tensor(own[t][:], tanh_vt[t][:], 1.0 / 0.3, tanh_slip[t][:], ALU.add, ALU.mult)

        def feeders(cols, w3_mx):
            width = cols.stop - cols.start
            name = "hid%d" % cols.start
            flow = keep.tile([P, PACK, width], F32, name=name + "_flow")
            for t in range(PACK):
                window = tanh_vt[t][:].indirect(entries(nb_sb, cols))
                nc.scalar.activation(vn[t][:, cols], window, ACT.Copy, bias=0.8 * 0.3, scale=0.8 * 0.3 * 0.3)
                nc.vector.scalar_tensor_tensor(
                    flow[:, t, :], vn[t][:, cols], unit_sb[:, t : t + 1], own[t][:, cols], ALU.mult, ALU.mult
                )
            grouped = keep.tile([P, width, PACK], BF16, name=name + "_grouped", align_bytes=64)
            nc.vector.tensor_tensor(
                by_fours(grouped[:]), rows_by_fours(damped[:, :, cols]), rows_by_fours(flow[:]), ALU.add
            )
            hid_mx = quantize(name, grouped[:].rearrange("p c t -> p (c t)"), width)
            acc = psum.tile([P, width], F32, name="acc", bufs=2)
            multiply(acc[:], w3_mx, slice(0, N), hid_mx, slice(0, width))
            result = keep.tile([P, width], F32, name=name + "_result")
            nc.scalar.copy(out=result[:], in_=acc[:])
            nc.scalar.dma_start(out=out[:, cols], in_=result[:])

        power(0)
        power(1)
        neighbour_freqs(0)
        slip(0)
        w2_mx = quantize("w2", dealt_weight("w2", w_raw[1], (nc.vector.tensor_copy,)), H)
        for t in range(1, PACK):
            if t + 1 < PACK:
                power(t + 1)
            neighbour_freqs(t)
            slip_terms(t - 1)
            slip(t)
        slip_terms(PACK - 1)
        w3_grouped = keep.tile([P, N, PACK], BF16, name="w3_grouped", align_bytes=64)
        nc.vector.tensor_copy(out=by_fours(w3_grouped[:]), in_=rows_by_fours(w3_raw[:]))
        w3_mx = quantize("w3", w3_grouped[:].rearrange("p n j -> p (n j)"), N)
        for t in range(PACK):
            voltage(t, w2_mx)
        for cols in PIECES:
            feeders(cols, w3_mx)
